import numpy as np
import ml_dtypes


def mxq(x, axis, fmt="e4m3"):
    dtype, down = {"e4m3": (ml_dtypes.float8_e4m3fn, 7), "e5m2": (ml_dtypes.float8_e5m2, 14)}[fmt]
    v = np.moveaxis(np.asarray(x, np.float32).astype(ml_dtypes.bfloat16).astype(np.float64), axis, -1)
    blocks = v.reshape(v.shape[:-1] + (-1, 32))
    amax = np.abs(blocks).max(-1, keepdims=True)
    byte = np.maximum(np.where(amax > 0, np.frexp(amax)[1] - 1 + 127, 0) - down, 1)
    scale = np.exp2(byte - 127.0)
    codes = (blocks / scale).astype(np.float32).astype(dtype).astype(np.float64)
    return np.moveaxis((codes * scale).reshape(v.shape), -1, axis)


WIDE = False


def mx_kscale(k):
    if not WIDE:
        return np.ones(k)
    levels = np.array([10, -10, 5, -5, 0])
    if k % 512:
        return np.exp2(np.random.permutation(np.resize(levels, k // 32))).repeat(32)
    a = np.empty((k // 512, 16))
    for p in range(k // 512):
        a[p, :8] = np.random.permutation(np.resize(levels, 8))
        for g in range(8):
            far = levels[np.abs(levels - a[p, g]) >= 10]
            a[p, g + 8] = far[np.random.randint(len(far))]
    return np.exp2(a.ravel()).repeat(32)


def f64(x):
    return np.asarray(x).astype(np.float64)


def striped(idx):
    return np.tile(idx.reshape(-1, 16).T, (8, 1)).astype(np.uint16)


def unstriped(offs):
    return offs[:16].T.reshape(-1).astype(np.int64)


def pack_weight(w):
    k, n = w.shape
    w = f64(np.asarray(w, np.float32).astype(ml_dtypes.bfloat16)).reshape(k // 32, 32, n)
    amax = np.abs(w).max(1)
    byte = np.clip(np.where(amax > 0, np.frexp(amax)[1] - 1 + 127 - 7, 1), 1, 254)
    scaled = (w * np.exp2(127.0 - byte)[:, None, :]).reshape(k, n).astype(np.float32)
    words = np.ascontiguousarray(scaled.reshape(k // 512, 128, 4, n).transpose(0, 1, 3, 2)).astype(ml_dtypes.float8_e4m3fn).view(np.uint8)
    return words, np.ascontiguousarray(byte.astype(np.uint8).reshape(k // 512, 16, n))


def unpack_weight(words, scales):
    g, p, n, _ = words.shape
    vals = np.ascontiguousarray(words).view(ml_dtypes.float8_e4m3fn).astype(np.float64) * np.repeat(np.exp2(scales.astype(np.float64) - 127.0), 8, axis=1)[..., None]
    return vals.transpose(0, 1, 3, 2).reshape(g * 512, n)


def sigmoid(v):
    return 1.0 / (1.0 + np.exp(-np.maximum(v, -700.0)))


def silu(v):
    return v / (1.0 + np.exp(-np.maximum(v, -700.0)))


K, T, S, H, N, W = 512, 2048, 512, 512, 256, 2048


def setup_inputs():
    n = np.random.standard_normal
    s = mx_kscale(K)[:, None]
    u = mx_kscale(H)
    packed_xT = pack_weight(n((K, T)) * s)
    packed_eT = pack_weight(n((K, W)) * s)
    return {
        "x_words": packed_xT[0],
        "x_scales": packed_xT[1],
        "e_words": packed_eT[0],
        "e_scales": packed_eT[1],
        "wk1": (n((K, H)) / np.sqrt(2 * K) / s).astype(np.float32),
        "wk2": (n((K, H)) / np.sqrt(2 * K) / s).astype(np.float32),
        "wv1": (n((K, H)) / np.sqrt(2 * K) / s).astype(np.float32),
        "wv2": (n((K, H)) / np.sqrt(2 * K) / s).astype(np.float32),
        "hid": (n((H, S))).astype(np.float32),
        "unit": (np.random.uniform(0.5, 1.5, (H, 1)) * u[:, None]).astype(np.float32),
        "wo": (n((H, N)) / np.sqrt(H) / u[:, None]).astype(np.float32),
        "skip": (n((N, S))).astype(np.float32),
        "offs": striped(np.random.permutation(T)[:S]),
        "tri": striped(np.random.permutation(W)[:S]),
    }


def reference(x_words, x_scales, e_words, e_scales, wk1, wk2, wv1, wv2, hid, unit, wo, skip, offs, tri):
    xq = unpack_weight(x_words, x_scales)[:, unstriped(offs)]
    e_tri = unpack_weight(e_words, e_scales)[:, unstriped(tri)]
    key = mxq(f64(wk1), 0, "e4m3").T @ xq + mxq(f64(wk2), 0, "e4m3").T @ e_tri
    gt = sigmoid(1.5 * (key * f64(hid)))
    val = mxq(f64(wv1), 0, "e4m3").T @ xq + mxq(f64(wv2), 0, "e4m3").T @ e_tri
    gv = gt * val
    cv = gv + 0.8 * (silu(0.6 * (np.pad(gv, ((0, 0), (1, 0)))[:, :S]) + gv))
    zz = f64(unit) * cv
    return (mxq(f64(wo), 0, "e4m3").T @ mxq(zz, 0, "e4m3")) + f64(skip)

@@ -1,0 +1,241 @@
+from contextlib import ExitStack
+
+import concourse.mybir as mybir
+
+K, T, S, H, N = 512, 2048, 512, 512, 256
+FLOPS = 2 * S * H * (4 * K + N)
+
+F32 = mybir.dt.float32
+BF16 = mybir.dt.bfloat16
+I32 = mybir.dt.int32
+U32 = mybir.dt.uint32
+U16 = mybir.dt.uint16
+U8 = mybir.dt.uint8
+FP8X4 = mybir.dt.float8_e4m3fn_x4
+ACT = mybir.ActivationFunctionType
+ALU = mybir.AluOpType
+
+P = 128
+PACK = 4
+PAD = 8
+CHUNKS = [(0, 128), (128, 256), (256, 384), (384, 512)]
+
+
+def tile_picked_yengrm_conv_p_kernel(
+    tc, x_words, x_scales, e_words, e_scales, wk1, wk2, wv1, wv2, hid, unit, wo, skip, offs, tri, out
+):
+    nc = tc.nc
+    with ExitStack() as ctx:
+        keep = ctx.enter_context(tc.tile_pool(name="keep", bufs=1))
+        psum = ctx.enter_context(tc.psum_pool(name="psum", bufs=1))
+
+        def sb(name, shape, dtype):
+            return keep.tile(shape, dtype, name=name, align_bytes=64)
+
+        offs_sb = keep.tile([P, S // 16], U16, name="offs_sb")
+        tri_sb = keep.tile([P, S // 16], U16, name="tri_sb")
+        xs_tab = sb("xs_tab", [P, T], U8)
+        es_tab = sb("es_tab", [P, T], U8)
+        xw_tab = sb("xw_tab", [P, T], I32)
+        ew_tab = sb("ew_tab", [P, T], I32)
+        zero = sb("zero", [P, PACK], F32)
+        g2 = sb("g2", [P, PACK, PAD + S], F32)
+
+        for tab in (xs_tab, es_tab):
+            nc.gpsimd.memset(tab[:, : T // 2].bitcast(I32), 0)
+            nc.vector.memset(tab[:, T // 2 :].bitcast(I32), 0)
+        nc.vector.memset(zero[:], 0.0)
+        nc.scalar.activation(out=g2[:, :, PAD - 1], in_=zero[:], func=ACT.Silu)
+
+        def load_rows(name, w, c0, c1):
+            raw = sb(name, [P, PACK, c1 - c0], F32)
+            nc.sync.dma_start(out=raw[:], in_=w.rearrange("(p j) c -> p j c", j=PACK)[:, :, c0:c1])
+            return raw
+
+        def load_words(tab, words):
+            nc.sync.dma_start(out=tab[:], in_=words[0].rearrange("p n t -> p (n t)").bitcast(I32))
+
+        def load_scales(queue, tab, scales):
+            for q in range(4):
+                queue.dma_start(
+                    out=tab[32 * q : 32 * q + 4, :].bitcast(I32), in_=scales[0, 4 * q : 4 * q + 4, :].bitcast(I32)
+                )
+
+        wk1_raw = load_rows("wk1_raw", wk1, 0, H)
+        nc.sync.dma_start(offs_sb[:], offs)
+        nc.sync.dma_start(tri_sb[:], tri)
+        load_words(xw_tab, x_words)
+        unit_sb = sb("unit_sb", [P, PACK], F32)
+        nc.sync.dma_start(out=unit_sb[:], in_=unit.rearrange("(p t) o -> p (t o)", t=PACK))
+        load_scales(nc.sync, xs_tab, x_scales)
+        load_words(ew_tab, e_words)
+        load_scales(nc.sync, es_tab, e_scales)
+        wk2_raw = load_rows("wk2_raw", wk2, 0, H)
+        wv1_raw = load_rows("wv1_raw", wv1, 0, H)
+
+        def load_hid(t):
+            h = sb("hid%d" % t, [P, S], F32)
+            nc.sync.dma_start(out=h[:], in_=hid.rearrange("(p t) j -> p t j", t=PACK)[:, t, :])
+            return h
+
+        hid_sb = [load_hid(t) for t in range(PACK - 1)]
+        wv2_lo = load_rows("wv2_lo", wv2, 0, H // 2)
+        wv2_hi = load_rows("wv2_hi", wv2, H // 2, H)
+        hid_sb.append(load_hid(PACK - 1))
+        wo_raw = load_rows("wo_raw", wo, 0, N)
+        skip_sb = sb("skip_sb", [P, N // P, S], F32)
+        nc.sync.dma_start(out=skip_sb[:], in_=skip.rearrange("(h p) j -> p h j", p=P))
+
+        def gather(name, tab, lst, dtype):
+            picked = sb(name, [P, S], dtype)
+            nc.vector.tensor_copy(out=picked[:], in_=tab.indirect(lst[:]))
+            return picked
+
+        def deal(copy, grouped, raw, m0, m1, r0):
+            copy(
+                out=grouped[:, :, m0:m1, :].rearrange("p t m j -> p m j t"),
+                in_=raw[:].rearrange("p j (m t) -> p m j t", t=PACK)[:, m0 - r0 : m1 - r0, :, :],
+            )
+
+        def quantize(name, grouped, width, pieces):
+            codes = sb(name + "_codes", [P, width], U32)
+            scales = sb(name + "_scales", [P, width], U8)
+            step = width // pieces
+            for c in range(0, width, step):
+                nc.vector.quantize_mx(
+                    out=codes[:, c : c + step].bitcast(FP8X4),
+                    scales=scales[:, c : c + step],
+                    in_=grouped[:, PACK * c : PACK * (c + step)],
+                )
+            return codes, scales
+
+        def mm(acc, w, cols, mov, start, stop):
+            nc.tensor.matmul_mx(
+                out=acc,
+                lhsT=w[0][:, cols].bitcast(FP8X4),
+                lhsT_scale=w[1][:, cols],
+                rhs=mov[0].bitcast(FP8X4),
+                rhs_scale=mov[1],
+                start=start,
+                stop=stop,
+            )
+
+        def flat(grouped):
+            return grouped[:].rearrange("p t m j -> p (t m j)")
+
+        grp = {n: sb(n + "_grp", [P, PACK, P, PACK], BF16) for n in ("wk1", "wk2", "wv1", "wv2")}
+        key = [psum.tile([P, S], F32, name="key%d" % t, tag="key%d" % t) for t in range(PACK)]
+        val = [psum.tile([P, S], F32, name="val%d" % t, tag="val%d" % t) for t in range(PACK)]
+        tcols = [slice(P * t, P * (t + 1)) for t in range(PACK)]
+
+        deal(nc.scalar.copy, grp["wk1"], wk1_raw, 0, P, 0)
+        xs = gather("xs", xs_tab[:], offs_sb, U8)
+        xw = gather("xw", xw_tab[:].bitcast(U32), offs_sb, U32)
+        q_wk1 = quantize("wk1", flat(grp["wk1"]), H, 1)
+        xq = (xw[:], xs[:])
+        for t in range(PACK):
+            mm(key[t][:], q_wk1, tcols[t], xq, True, False)
+        ew = gather("ew", ew_tab[:].bitcast(U32), tri_sb, U32)
+        es = gather("es", es_tab[:], tri_sb, U8)
+        deal(nc.scalar.copy, grp["wk2"], wk2_raw, 0, 48, 0)
+        deal(nc.vector.tensor_copy, grp["wk2"], wk2_raw, 48, P, 0)
+        q_wk2 = quantize("wk2", flat(grp["wk2"]), H, PACK)
+        eq = (ew[:], es[:])
+        for t in range(PACK):
+            mm(key[t][:], q_wk2, tcols[t], eq, False, True)
+        deal(nc.scalar.copy, grp["wv1"], wv1_raw, 0, P, 0)
+        q_wv1 = quantize("wv1", flat(grp["wv1"]), H, 1)
+        for t in range(PACK):
+            mm(val[t][:], q_wv1, tcols[t], xq, True, False)
+
+        def gate(t):
+            kh = sb("kh%d" % t, [P, S], F32)
+            nc.vector.tensor_tensor(out=kh[:], in0=key[t][:], in1=hid_sb[t][:], op=ALU.mult)
+            tht = sb("th%d" % t, [P, S], F32)
+            nc.scalar.activation(out=tht[:], in_=kh[:], func=ACT.Tanh, scale=0.75)
+            return tht
+
+        th = [gate(t) for t in range(PACK - 1)]
+        deal(nc.vector.tensor_copy, grp["wv2"], wv2_lo, 0, P // 2, 0)
+        deal(nc.vector.tensor_copy, grp["wv2"], wv2_hi, P // 2, 104, P // 2)
+        deal(nc.scalar.copy, grp["wv2"], wv2_hi, 104, P, P // 2)
+        q_wv2 = quantize("wv2", flat(grp["wv2"]), H, PACK)
+        for t in range(PACK):
+            mm(val[t][:], q_wv2, tcols[t], eq, False, True)
+        th.append(gate(PACK - 1))
+
+        ua = sb("ua", [P, PACK], F32)
+        ub = sb("ub", [P, PACK], F32)
+        nc.gpsimd.tensor_scalar(out=ua[:], in0=unit_sb[:], scalar1=0.5, scalar2=None, op0=ALU.mult)
+        nc.gpsimd.tensor_scalar(out=ub[:], in0=unit_sb[:], scalar1=0.8, scalar2=None, op0=ALU.mult)
+
+        wo_grp = sb("wo_grp", [P, N, PACK], BF16)
+
+        nc.scalar.copy(
+            out=wo_grp[:].rearrange("p (c i) j -> p c j i", i=4),
+            in_=wo_raw[:].rearrange("p j (c i) -> p c j i", i=4),
+        )
+        sl, ga = [], []
+        for t in range(PACK):
+            nc.vector.scalar_tensor_tensor(
+                out=g2[:, t, PAD:], in0=th[t][:], scalar=1.0, in1=val[t][:], op0=ALU.add, op1=ALU.mult
+            )
+            u2 = sb("u2_%d" % t, [P, S], F32)
+            nc.vector.scalar_tensor_tensor(
+                out=u2[:], in0=g2[:, t, PAD - 1 : PAD - 1 + S], scalar=0.6, in1=g2[:, t, PAD:],
+                op0=ALU.mult, op1=ALU.add,
+            )
+            gat = sb("ga%d" % t, [P, S], F32)
+            nc.scalar.activation(out=gat[:], in_=g2[:, t, PAD:], func=ACT.Copy, scale=ua[:, t : t + 1])
+            slt = sb("sl%d" % t, [P, S], F32)
+            nc.scalar.activation(out=slt[:], in_=u2[:], func=ACT.Silu, scale=0.5)
+            sl.append(slt)
+            ga.append(gat)
+        q_wo = quantize("wo", wo_grp[:].rearrange("p n j -> p (n j)"), N, 1)
+        z32 = sb("z32", [P, PACK, S], F32)
+
+        def mix(j0, j1):
+            for t in range(PACK):
+                nc.vector.scalar_tensor_tensor(
+                    out=z32[:, t, j0:j1], in0=sl[t][:, j0:j1], scalar=ub[:, t : t + 1], in1=ga[t][:, j0:j1],
+                    op0=ALU.mult, op1=ALU.add,
+                )
+
+        acc = {}
+
+        def weave(c):
+            j0, j1 = CHUNKS[c]
+            zz = sb("zz%d" % c, [P, j1 - j0, PACK], BF16)
+            copy = nc.vector.tensor_copy if c == 3 else nc.scalar.copy
+            copy(
+                out=zz[:].rearrange("p (c i) t -> p c t i", i=4),
+                in_=z32[:, :, j0:j1].rearrange("p t (c i) -> p c t i", i=4),
+            )
+            return zz
+
+        def product(c, zz):
+            j0, j1 = CHUNKS[c]
+            w = j1 - j0
+            zq = quantize("zz%d" % c, zz[:].rearrange("p j t -> p (j t)"), w, 1)
+            acc[c] = psum.tile([P, N // P, w], F32, name="acc%d" % c, tag="key%d" % c)
+            for h in range(N // P):
+                mm(acc[c][:, h, :], q_wo, tcols[h], (zq[0][:], zq[1][:]), True, True)
+
+        def finish(c):
+            j0, j1 = CHUNKS[c]
+            res = sb("res%d" % c, [P, N // P, j1 - j0], F32)
+            nc.vector.tensor_tensor(out=res[:], in0=acc[c][:], in1=skip_sb[:, :, j0:j1], op=ALU.add)
+            nc.sync.dma_start(out=out.rearrange("(h p) j -> p h j", p=P)[:, :, j0:j1], in_=res[:])
+
+        mix(0, S // 2)
+        zzs = [weave(0), weave(1)]
+        mix(S // 2, S)
+        zzs.extend([weave(2), weave(3)])
+        product(0, zzs[0])
+        product(1, zzs[1])
+        product(3, zzs[3])
+        finish(0)
+        product(2, zzs[2])
+        finish(1)
+        finish(3)
+        finish(2)

@@ -55,10 +55,10 @@ def tile_picked_yengrm_conv_p_kernel(
         def load_words(tab, words):
             nc.sync.dma_start(out=tab[:], in_=words[0].rearrange("p n t -> p (n t)").bitcast(I32))
 
-        def load_scales(queue, tab, scales):
-            for q in range(4):
-                queue.dma_start(
-                    out=tab[32 * q : 32 * q + 4, :].bitcast(I32), in_=scales[0, 4 * q : 4 * q + 4, :].bitcast(I32)
+        def load_scales(tab, scales, first):
+            for r in range(4):
+                nc.sync.dma_start(
+                    out=tab[first + r : P : 32, :].bitcast(I32), in_=scales[0, r:16:4, :].bitcast(I32)
                 )
 
         wk1_raw = load_rows("wk1_raw", wk1, 0, H)
@@ -67,21 +67,20 @@ def tile_picked_yengrm_conv_p_kernel(
         load_words(xw_tab, x_words)
         unit_sb = sb("unit_sb", [P, PACK], F32)
         nc.sync.dma_start(out=unit_sb[:], in_=unit.rearrange("(p t) o -> p (t o)", t=PACK))
-        load_scales(nc.sync, xs_tab, x_scales)
+        load_scales(xs_tab, x_scales, 0)
         load_words(ew_tab, e_words)
-        load_scales(nc.sync, es_tab, e_scales)
+        load_scales(es_tab, e_scales, 4)
         wk2_raw = load_rows("wk2_raw", wk2, 0, H)
         wv1_raw = load_rows("wv1_raw", wv1, 0, H)
 
         def load_hid(t):
             h = sb("hid%d" % t, [P, S], F32)
             nc.sync.dma_start(out=h[:], in_=hid.rearrange("(p t) j -> p t j", t=PACK)[:, t, :])
-            return h
+            return h[:]
 
-        hid_sb = [load_hid(t) for t in range(PACK - 1)]
+        hid_sb = [load_hid(t) for t in range(PACK)]
         wv2_lo = load_rows("wv2_lo", wv2, 0, H // 2)
         wv2_hi = load_rows("wv2_hi", wv2, H // 2, H)
-        hid_sb.append(load_hid(PACK - 1))
         wo_raw = load_rows("wo_raw", wo, 0, N)
         skip_sb = sb("skip_sb", [P, N // P, S], F32)
         nc.sync.dma_start(out=skip_sb[:], in_=skip.rearrange("(h p) j -> p h j", p=P))
@@ -140,29 +139,29 @@ def tile_picked_yengrm_conv_p_kernel(
         deal(nc.scalar.copy, grp["wk2"], wk2_raw, 0, 48, 0)
         deal(nc.vector.tensor_copy, grp["wk2"], wk2_raw, 48, P, 0)
         q_wk2 = quantize("wk2", flat(grp["wk2"]), H, PACK)
-        eq = (ew[:], es[:])
+        eq = (ew[:], es[4:P, :])
         for t in range(PACK):
             mm(key[t][:], q_wk2, tcols[t], eq, False, True)
-        deal(nc.scalar.copy, grp["wv1"], wv1_raw, 0, P, 0)
+        deal(nc.scalar.copy, grp["wv1"], wv1_raw, 0, P // 2, 0)
+        deal(nc.vector.tensor_copy, grp["wv1"], wv1_raw, P // 2, P, 0)
         q_wv1 = quantize("wv1", flat(grp["wv1"]), H, 1)
         for t in range(PACK):
             mm(val[t][:], q_wv1, tcols[t], xq, True, False)
 
         def gate(t):
             kh = sb("kh%d" % t, [P, S], F32)
-            nc.vector.tensor_tensor(out=kh[:], in0=key[t][:], in1=hid_sb[t][:], op=ALU.mult)
+            nc.vector.tensor_tensor(out=kh[:], in0=key[t][:], in1=hid_sb[t], op=ALU.mult)
             tht = sb("th%d" % t, [P, S], F32)
             nc.scalar.activation(out=tht[:], in_=kh[:], func=ACT.Tanh, scale=0.75)
             return tht
 
-        th = [gate(t) for t in range(PACK - 1)]
+        th = [gate(t) for t in range(PACK)]
         deal(nc.vector.tensor_copy, grp["wv2"], wv2_lo, 0, P // 2, 0)
         deal(nc.vector.tensor_copy, grp["wv2"], wv2_hi, P // 2, 104, P // 2)
         deal(nc.scalar.copy, grp["wv2"], wv2_hi, 104, P, P // 2)
         q_wv2 = quantize("wv2", flat(grp["wv2"]), H, PACK)
         for t in range(PACK):
             mm(val[t][:], q_wv2, tcols[t], eq, False, True)
-        th.append(gate(PACK - 1))
 
         ua = sb("ua", [P, PACK], F32)
         ub = sb("ub", [P, PACK], F32)
@@ -176,10 +175,16 @@ def tile_picked_yengrm_conv_p_kernel(
             in_=wo_raw[:].rearrange("p j (c i) -> p c j i", i=4),
         )
         sl, ga = [], []
-        for t in range(PACK):
+
+        def gated(t):
             nc.vector.scalar_tensor_tensor(
                 out=g2[:, t, PAD:], in0=th[t][:], scalar=1.0, in1=val[t][:], op0=ALU.add, op1=ALU.mult
             )
+
+        gated(0)
+        for t in range(PACK):
+            if t + 1 < PACK:
+                gated(t + 1)
             u2 = sb("u2_%d" % t, [P, S], F32)
             nc.vector.scalar_tensor_tensor(
                 out=u2[:], in0=g2[:, t, PAD - 1 : PAD - 1 + S], scalar=0.6, in1=g2[:, t, PAD:],

from contextlib import ExitStack

import concourse.mybir as mybir

K, T, S, H, N = 512, 2048, 512, 512, 256
FLOPS = 2 * S * H * (4 * K + N)

F32 = mybir.dt.float32
BF16 = mybir.dt.bfloat16
I32 = mybir.dt.int32
U32 = mybir.dt.uint32
U16 = mybir.dt.uint16
U8 = mybir.dt.uint8
FP8X4 = mybir.dt.float8_e4m3fn_x4
ACT = mybir.ActivationFunctionType
ALU = mybir.AluOpType

P = 128
PACK = 4
PAD = 8
CHUNKS = [(0, 128), (128, 256), (256, 384), (384, 512)]


def tile_picked_yengrm_conv_p_kernel(
    tc, x_words, x_scales, e_words, e_scales, wk1, wk2, wv1, wv2, hid, unit, wo, skip, offs, tri, out
):
    nc = tc.nc
    with ExitStack() as ctx:
        keep = ctx.enter_context(tc.tile_pool(name="keep", bufs=1))
        psum = ctx.enter_context(tc.psum_pool(name="psum", bufs=1))

        def sb(name, shape, dtype):
            return keep.tile(shape, dtype, name=name, align_bytes=64)

        offs_sb = keep.tile([P, S // 16], U16, name="offs_sb")
        tri_sb = keep.tile([P, S // 16], U16, name="tri_sb")
        xs_tab = sb("xs_tab", [P, T], U8)
        es_tab = sb("es_tab", [P, T], U8)
        xw_tab = sb("xw_tab", [P, T], I32)
        ew_tab = sb("ew_tab", [P, T], I32)
        zero = sb("zero", [P, PACK], F32)
        g2 = sb("g2", [P, PACK, PAD + S], F32)

        for tab in (xs_tab, es_tab):
            nc.gpsimd.memset(tab[:, : T // 2].bitcast(I32), 0)
            nc.vector.memset(tab[:, T // 2 :].bitcast(I32), 0)
        nc.vector.memset(zero[:], 0.0)
        nc.scalar.activation(out=g2[:, :, PAD - 1], in_=zero[:], func=ACT.Silu)

        def load_rows(name, w, c0, c1):
            raw = sb(name, [P, PACK, c1 - c0], F32)
            nc.sync.dma_start(out=raw[:], in_=w.rearrange("(p j) c -> p j c", j=PACK)[:, :, c0:c1])
            return raw

        def load_words(tab, words):
            nc.sync.dma_start(out=tab[:], in_=words[0].rearrange("p n t -> p (n t)").bitcast(I32))

        def load_scales(tab, scales, first):
            for r in range(4):
                nc.sync.dma_start(
                    out=tab[first + r : P : 32, :].bitcast(I32), in_=scales[0, r:16:4, :].bitcast(I32)
                )

        wk1_raw = load_rows("wk1_raw", wk1, 0, H)
        nc.sync.dma_start(offs_sb[:], offs)
        nc.sync.dma_start(tri_sb[:], tri)
        load_words(xw_tab, x_words)
        unit_sb = sb("unit_sb", [P, PACK], F32)
        nc.sync.dma_start(out=unit_sb[:], in_=unit.rearrange("(p t) o -> p (t o)", t=PACK))
        load_scales(xs_tab, x_scales, 0)
        load_words(ew_tab, e_words)
        load_scales(es_tab, e_scales, 4)
        wk2_raw = load_rows("wk2_raw", wk2, 0, H)
        wv1_raw = load_rows("wv1_raw", wv1, 0, H)

        def load_hid(t):
            h = sb("hid%d" % t, [P, S], F32)
            nc.sync.dma_start(out=h[:], in_=hid.rearrange("(p t) j -> p t j", t=PACK)[:, t, :])
            return h[:]

        hid_sb = [load_hid(t) for t in range(PACK)]
        wv2_lo = load_rows("wv2_lo", wv2, 0, H // 2)
        wv2_hi = load_rows("wv2_hi", wv2, H // 2, H)
        wo_raw = load_rows("wo_raw", wo, 0, N)
        skip_sb = sb("skip_sb", [P, N // P, S], F32)
        nc.sync.dma_start(out=skip_sb[:], in_=skip.rearrange("(h p) j -> p h j", p=P))

        def gather(name, tab, lst, dtype):
            picked = sb(name, [P, S], dtype)
            nc.vector.tensor_copy(out=picked[:], in_=tab.indirect(lst[:]))
            return picked

        def deal(copy, grouped, raw, m0, m1, r0):
            copy(
                out=grouped[:, :, m0:m1, :].rearrange("p t m j -> p m j t"),
                in_=raw[:].rearrange("p j (m t) -> p m j t", t=PACK)[:, m0 - r0 : m1 - r0, :, :],
            )

        def quantize(name, grouped, width, pieces):
            codes = sb(name + "_codes", [P, width], U32)
            scales = sb(name + "_scales", [P, width], U8)
            step = width // pieces
            for c in range(0, width, step):
                nc.vector.quantize_mx(
                    out=codes[:, c : c + step].bitcast(FP8X4),
                    scales=scales[:, c : c + step],
                    in_=grouped[:, PACK * c : PACK * (c + step)],
                )
            return codes, scales

        def mm(acc, w, cols, mov, start, stop):
            nc.tensor.matmul_mx(
                out=acc,
                lhsT=w[0][:, cols].bitcast(FP8X4),
                lhsT_scale=w[1][:, cols],
                rhs=mov[0].bitcast(FP8X4),
                rhs_scale=mov[1],
                start=start,
                stop=stop,
            )

        def flat(grouped):
            return grouped[:].rearrange("p t m j -> p (t m j)")

        grp = {n: sb(n + "_grp", [P, PACK, P, PACK], BF16) for n in ("wk1", "wk2", "wv1", "wv2")}
        key = [psum.tile([P, S], F32, name="key%d" % t, tag="key%d" % t) for t in range(PACK)]
        val = [psum.tile([P, S], F32, name="val%d" % t, tag="val%d" % t) for t in range(PACK)]
        tcols = [slice(P * t, P * (t + 1)) for t in range(PACK)]

        deal(nc.scalar.copy, grp["wk1"], wk1_raw, 0, P, 0)
        xs = gather("xs", xs_tab[:], offs_sb, U8)
        xw = gather("xw", xw_tab[:].bitcast(U32), offs_sb, U32)
        q_wk1 = quantize("wk1", flat(grp["wk1"]), H, 1)
        xq = (xw[:], xs[:])
        for t in range(PACK):
            mm(key[t][:], q_wk1, tcols[t], xq, True, False)
        ew = gather("ew", ew_tab[:].bitcast(U32), tri_sb, U32)
        es = gather("es", es_tab[:], tri_sb, U8)
        deal(nc.scalar.copy, grp["wk2"], wk2_raw, 0, 48, 0)
        deal(nc.vector.tensor_copy, grp["wk2"], wk2_raw, 48, P, 0)
        q_wk2 = quantize("wk2", flat(grp["wk2"]), H, PACK)
        eq = (ew[:], es[4:P, :])
        for t in range(PACK):
            mm(key[t][:], q_wk2, tcols[t], eq, False, True)
        deal(nc.scalar.copy, grp["wv1"], wv1_raw, 0, P // 2, 0)
        deal(nc.vector.tensor_copy, grp["wv1"], wv1_raw, P // 2, P, 0)
        q_wv1 = quantize("wv1", flat(grp["wv1"]), H, 1)
        for t in range(PACK):
            mm(val[t][:], q_wv1, tcols[t], xq, True, False)

        def gate(t):
            kh = sb("kh%d" % t, [P, S], F32)
            nc.vector.tensor_tensor(out=kh[:], in0=key[t][:], in1=hid_sb[t], op=ALU.mult)
            tht = sb("th%d" % t, [P, S], F32)
            nc.scalar.activation(out=tht[:], in_=kh[:], func=ACT.Tanh, scale=0.75)
            return tht

        th = [gate(t) for t in range(PACK)]
        deal(nc.vector.tensor_copy, grp["wv2"], wv2_lo, 0, P // 2, 0)
        deal(nc.vector.tensor_copy, grp["wv2"], wv2_hi, P // 2, 104, P // 2)
        deal(nc.scalar.copy, grp["wv2"], wv2_hi, 104, P, P // 2)
        q_wv2 = quantize("wv2", flat(grp["wv2"]), H, PACK)
        for t in range(PACK):
            mm(val[t][:], q_wv2, tcols[t], eq, False, True)

        ua = sb("ua", [P, PACK], F32)
        ub = sb("ub", [P, PACK], F32)
        nc.gpsimd.tensor_scalar(out=ua[:], in0=unit_sb[:], scalar1=0.5, scalar2=None, op0=ALU.mult)
        nc.gpsimd.tensor_scalar(out=ub[:], in0=unit_sb[:], scalar1=0.8, scalar2=None, op0=ALU.mult)

        wo_grp = sb("wo_grp", [P, N, PACK], BF16)

        nc.scalar.copy(
            out=wo_grp[:].rearrange("p (c i) j -> p c j i", i=4),
            in_=wo_raw[:].rearrange("p j (c i) -> p c j i", i=4),
        )
        sl, ga = [], []

        def gated(t):
            nc.vector.scalar_tensor_tensor(
                out=g2[:, t, PAD:], in0=th[t][:], scalar=1.0, in1=val[t][:], op0=ALU.add, op1=ALU.mult
            )

        gated(0)
        for t in range(PACK):
            if t + 1 < PACK:
                gated(t + 1)
            u2 = sb("u2_%d" % t, [P, S], F32)
            nc.vector.scalar_tensor_tensor(
                out=u2[:], in0=g2[:, t, PAD - 1 : PAD - 1 + S], scalar=0.6, in1=g2[:, t, PAD:],
                op0=ALU.mult, op1=ALU.add,
            )
            gat = sb("ga%d" % t, [P, S], F32)
            nc.scalar.activation(out=gat[:], in_=g2[:, t, PAD:], func=ACT.Copy, scale=ua[:, t : t + 1])
            slt = sb("sl%d" % t, [P, S], F32)
            nc.scalar.activation(out=slt[:], in_=u2[:], func=ACT.Silu, scale=0.5)
            sl.append(slt)
            ga.append(gat)
        q_wo = quantize("wo", wo_grp[:].rearrange("p n j -> p (n j)"), N, 1)
        z32 = sb("z32", [P, PACK, S], F32)

        def mix(j0, j1):
            for t in range(PACK):
                nc.vector.scalar_tensor_tensor(
                    out=z32[:, t, j0:j1], in0=sl[t][:, j0:j1], scalar=ub[:, t : t + 1], in1=ga[t][:, j0:j1],
                    op0=ALU.mult, op1=ALU.add,
                )

        acc = {}

        def weave(c):
            j0, j1 = CHUNKS[c]
            zz = sb("zz%d" % c, [P, j1 - j0, PACK], BF16)
            copy = nc.vector.tensor_copy if c == 3 else nc.scalar.copy
            copy(
                out=zz[:].rearrange("p (c i) t -> p c t i", i=4),
                in_=z32[:, :, j0:j1].rearrange("p t (c i) -> p c t i", i=4),
            )
            return zz

        def product(c, zz):
            j0, j1 = CHUNKS[c]
            w = j1 - j0
            zq = quantize("zz%d" % c, zz[:].rearrange("p j t -> p (j t)"), w, 1)
            acc[c] = psum.tile([P, N // P, w], F32, name="acc%d" % c, tag="key%d" % c)
            for h in range(N // P):
                mm(acc[c][:, h, :], q_wo, tcols[h], (zq[0][:], zq[1][:]), True, True)

        def finish(c):
            j0, j1 = CHUNKS[c]
            res = sb("res%d" % c, [P, N // P, j1 - j0], F32)
            nc.vector.tensor_tensor(out=res[:], in0=acc[c][:], in1=skip_sb[:, :, j0:j1], op=ALU.add)
            nc.sync.dma_start(out=out.rearrange("(h p) j -> p h j", p=P)[:, :, j0:j1], in_=res[:])

        mix(0, S // 2)
        zzs = [weave(0), weave(1)]
        mix(S // 2, S)
        zzs.extend([weave(2), weave(3)])
        product(0, zzs[0])
        product(1, zzs[1])
        product(3, zzs[3])
        finish(0)
        product(2, zzs[2])
        finish(1)
        finish(3)
        finish(2)
